import numpy as np
import ml_dtypes


def mxq(x, axis, fmt="e4m3"):
    dtype, down = {"e4m3": (ml_dtypes.float8_e4m3fn, 7), "e5m2": (ml_dtypes.float8_e5m2, 14)}[fmt]
    v = np.moveaxis(np.asarray(x, np.float32).astype(ml_dtypes.bfloat16).astype(np.float64), axis, -1)
    blocks = v.reshape(v.shape[:-1] + (-1, 32))
    amax = np.abs(blocks).max(-1, keepdims=True)
    byte = np.maximum(np.where(amax > 0, np.frexp(amax)[1] - 1 + 127, 0) - down, 1)
    scale = np.exp2(byte - 127.0)
    codes = (blocks / scale).astype(np.float32).astype(dtype).astype(np.float64)
    return np.moveaxis((codes * scale).reshape(v.shape), -1, axis)


WIDE = False


def mx_kscale(k):
    if not WIDE:
        return np.ones(k)
    levels = np.array([10, -10, 5, -5, 0])
    if k % 512:
        return np.exp2(np.random.permutation(np.resize(levels, k // 32))).repeat(32)
    a = np.empty((k // 512, 16))
    for p in range(k // 512):
        a[p, :8] = np.random.permutation(np.resize(levels, 8))
        for g in range(8):
            far = levels[np.abs(levels - a[p, g]) >= 10]
            a[p, g + 8] = far[np.random.randint(len(far))]
    return np.exp2(a.ravel()).repeat(32)


def f64(x):
    return np.asarray(x).astype(np.float64)


def striped(idx):
    return np.tile(idx.reshape(-1, 16).T, (8, 1)).astype(np.uint16)


def unstriped(offs):
    return offs[:16].T.reshape(-1).astype(np.int64)


E2M1 = np.array([0.0, 0.5, 1.0, 1.5, 2.0, 3.0, 4.0, 6.0, -0.0, -0.5, -1.0, -1.5, -2.0, -3.0, -4.0, -6.0])


def pack_weight(w, fmt):
    k, n = w.shape
    w = f64(np.asarray(w, np.float32).astype(ml_dtypes.bfloat16)).reshape(k // 32, 32, n)
    amax = np.abs(w).max(1)
    if fmt == "e4m3":
        byte = np.frexp(amax)[1] - 1 + 127 - 7
    else:
        mant, ex = np.frexp(amax / 6.0)
        byte = np.where(mant > 0.5, ex, ex - 1) + 127
    byte = np.clip(np.where(amax > 0, byte, 1), 1, 254)
    scaled = (w * np.exp2(127.0 - byte)[:, None, :]).reshape(k, n).astype(np.float32)
    by_word = np.ascontiguousarray(scaled.reshape(k // 512, 128, 4, n).transpose(0, 1, 3, 2))
    if fmt == "e4m3":
        words = by_word.astype(ml_dtypes.float8_e4m3fn).view(np.uint8)
    else:
        c = by_word.astype(ml_dtypes.float4_e2m1fn).view(np.uint8) & 0xF
        words = (c[..., 0::2] | (c[..., 1::2] << 4)).reshape(k // 512, 128, 2 * n)
    return np.ascontiguousarray(words), np.ascontiguousarray(byte.astype(np.uint8).reshape(k // 512, 16, n))


def unpack_weight(words, scales, fmt):
    g, _, n = scales.shape
    words = np.ascontiguousarray(words).reshape(g, 128, n, -1)
    if fmt == "e4m3":
        vals = words.view(ml_dtypes.float8_e4m3fn).astype(np.float64)
    else:
        nib = np.empty((g, 128, n, 4), np.uint8)
        nib[..., 0::2] = words & 0xF
        nib[..., 1::2] = words >> 4
        vals = E2M1[nib]
    vals = vals * np.repeat(np.exp2(scales.astype(np.float64) - 127.0), 8, axis=1)[..., None]
    return vals.transpose(0, 1, 3, 2).reshape(g * 512, n)


def gelu(v):
    return 0.5 * v * (1.0 + np.tanh(np.sqrt(2.0 / np.pi) * (v + 0.044715 * v**3)))


def striped8(idx):
    return np.concatenate([v.reshape(-1, 16).T for v in idx]).astype(np.uint16)


def unstriped8(offs):
    return np.stack([offs[16 * g:16 * g + 16].T.reshape(-1) for g in range(8)]).astype(np.int64)


def heads(h, wgt, idx8):
    r = np.arange(h.shape[0])
    return wgt[r // 4 % 128] * h[r[:, None], idx8[r % 512 // 64]]


def put_heads(h, wgs, idx8, t2):
    r = np.arange(h.shape[0])
    page = np.zeros((h.shape[0], t2))
    page[r[:, None], idx8[r % 512 // 64]] = wgs[r // 4 % 128] * h
    return page


K, H, N, T, S, P, T2 = 512, 1024, 384, 4096, 1024, 1024, 2048

def setup_inputs():
    n = np.random.standard_normal
    s = mx_kscale(K)[:, None]
    u = mx_kscale(H)[:, None]
    d = {}
    d["tab_words"], d["tab_scales"] = pack_weight(n((K, T)) * s, "e4m3")
    d["offs"] = striped(np.random.permutation(T)[:S])
    d["w1"] = (0.9 * n((K, H)) / K ** 0.5 / s).astype(np.float32)
    d["w2_words"], d["w2_scales"] = pack_weight(0.9 * n((K, H)) / K ** 0.5 / s, "e2m1")
    d["w3_words"], d["w3_scales"] = pack_weight(0.9 * n((K, H)) / K ** 0.5 / s, "e4m3")
    d["wgs"] = np.repeat(np.random.uniform(0.5, 2.0, (8, S)), 16, axis=0).astype(np.float32)
    d["offs2"] = striped8(np.stack([np.random.permutation(T2)[:S] for _ in range(8)]))
    d["wgt"] = np.repeat(np.random.uniform(0.5, 2.0, (8, P)), 16, axis=0).astype(np.float32)
    d["offs3"] = striped8(np.stack([np.random.permutation(T2)[:P] for _ in range(8)]))
    d["gain"] = (np.exp(0.3 * n(H)) * u[:, 0]).astype(np.float32)
    d["wear"] = (0.5 * n((H, P)) * u).astype(np.float32)
    d["w4"] = (1.5 * n((H, N)) / H ** 0.5 / u).astype(np.float32)
    return d

def reference(tab_words, tab_scales, offs, w1, w2_words, w2_scales, w3_words, w3_scales,
              wgs, offs2, wgt, offs3, gain, wear, w4):
    v = unpack_weight(tab_words, tab_scales, "e4m3")[:, unstriped(offs)]
    w2 = unpack_weight(w2_words, w2_scales, "e2m1")
    w3 = unpack_weight(w3_words, w3_scales, "e4m3")
    a = mxq(f64(w1), 0, "e4m3").T @ v
    b = w2.T @ v
    c = w3.T @ v
    h = np.maximum(a, b) - np.abs(c)
    page = put_heads(h, f64(wgs), unstriped8(offs2), T2)
    x = heads(page, f64(wgt), unstriped8(offs3))
    z = f64(gain)[:, None] * np.tanh(x) + f64(wear)
    out = mxq(f64(w4), 0, "e4m3").T @ mxq(z, 0, "e4m3")
    return out

@@ -1,0 +1,351 @@
+from contextlib import ExitStack
+
+import concourse.mybir as mybir
+from concourse.masks import make_identity
+
+K, H, N, T, S, M, T2 = 512, 1024, 384, 4096, 1024, 1024, 2048
+FLOPS = 2 * (3 * K * H * S + H * N * M)
+
+F32 = mybir.dt.float32
+BF16 = mybir.dt.bfloat16
+I32 = mybir.dt.int32
+U32 = mybir.dt.uint32
+U16 = mybir.dt.uint16
+U8 = mybir.dt.uint8
+FP8X4 = mybir.dt.float8_e4m3fn_x4
+FP4X4 = mybir.dt.float4_e2m1fn_x4
+ALU = mybir.AluOpType
+ACT = mybir.ActivationFunctionType
+
+P = 128
+PACK = 4
+BLOCK = P * PACK
+BANK = 512
+CHUNK = 256
+PER_COL = 16
+SPARE = 8
+SLOT = 4096
+
+
+def tile_list_banknote_pocket_scores_kernel(
+    tc, tab_words, tab_scales, offs, w1, w2_words, w2_scales, w3_words, w3_scales,
+    wgs, offs2, wgt, offs3, gain, wear, w4, out,
+):
+    nc = tc.nc
+    with ExitStack() as ctx:
+        keep = ctx.enter_context(tc.tile_pool(name="keep", bufs=1))
+        ring = ctx.enter_context(tc.tile_pool(name="ring", bufs=2))
+        shared = ctx.enter_context(tc.tile_pool(name="shared", bufs=1))
+        psum = ctx.enter_context(tc.psum_pool(name="psum", bufs=1))
+
+        def slot_tile(slot, shape, dtype, name):
+            return shared.tile(shape, dtype, name=name, offset=int(slot * SLOT), align_bytes=64)
+
+        def bank(shape, tag, name):
+            return psum.tile(shape, F32, name=name, tag=tag, bufs=1 if tag in "AC" else 2)
+
+        list1 = keep.tile([P, S // PER_COL], U16, name="list1")
+        list2 = keep.tile([P, S // PER_COL], U16, name="list2")
+        list3 = keep.tile([P, M // PER_COL], U16, name="list3")
+        table_scales = keep.tile([P, T], U8, name="table_scales", align_bytes=64)
+        w1_codes = slot_tile(7, [P, H], U32, "w1_codes")
+        w1_planes = keep.tile([P, H], U8, name="w1_planes", align_bytes=64)
+        w2_planes = keep.tile([P, H], U8, name="w2_planes", align_bytes=64)
+        w4_codes = keep.tile([P, 2 * N], U32, name="w4_codes", align_bytes=64)
+        w4_planes = keep.tile([P, 2 * N], U8, name="w4_planes", align_bytes=64)
+        z_codes = keep.tile([P, 2 * M], U32, name="z_codes", align_bytes=64)
+        z_planes = keep.tile([P, 2 * M], U8, name="z_planes", align_bytes=64)
+        gain_sb = keep.tile([P, 2, PACK], F32, name="gain_sb")
+        ident = keep.tile([P, P], F32, name="ident")
+        warm = slot_tile(3, [P, 8], F32, "warm")
+        pages = [keep.tile([P, T2 + SPARE], F32, name="page%d" % t) for t in range(PACK)]
+        v_words = [keep.tile([P, BANK], U32, name="v_words%d" % i, align_bytes=64) for i in range(2)]
+        v_scales = [keep.tile([P, BANK], U8, name="v_scales%d" % i, align_bytes=64) for i in range(2)]
+        h_rows = [keep.tile([P, PACK, S], F32, name="h_rows%d" % b) for b in range(2)]
+
+        def load_planes(queue, tile, src):
+            for q in range(4):
+                queue.dma_start(
+                    out=tile[32 * q : 32 * q + 4, :].bitcast(I32), in_=src[0, 4 * q : 4 * q + 4, :].bitcast(I32)
+                )
+
+        raw = {}
+
+        def load_rows(key, rows, slot):
+            width = rows.shape[1]
+            raw[key] = slot_tile(slot, [P, PACK, width], F32, "raw_%s%d" % key)
+            nc.sync.dma_start(out=raw[key][:], in_=rows.rearrange("(p i) w -> p i w", i=PACK))
+
+        grouped = {}
+
+        def round_rows(key, slot):
+            width = raw[key].shape[2]
+            grouped[key] = slot_tile(slot, [P, width * PACK], BF16, "grouped_%s%d" % key)
+            nc.scalar.copy(
+                grouped[key][:].rearrange("p (c e i) -> p c i e", e=4, i=PACK),
+                raw[key][:].rearrange("p i (c e) -> p c i e", e=4),
+            )
+
+        def quantise(codes, planes, col0, values, piece):
+            total = values.shape[1] // PACK
+            for done in range(0, total, piece):
+                n = min(piece, total - done)
+                cols = slice(col0 + done, col0 + done + n)
+                nc.vector.quantize_mx(
+                    out=codes[:, cols].bitcast(FP8X4),
+                    scales=planes[:, cols],
+                    in_=values[:, PACK * done : PACK * (done + n)],
+                )
+
+        w2_dram = w2_words[0].bitcast(I32)
+        w3_dram = w3_words[0].rearrange("p c i -> p (c i)").bitcast(I32)
+
+        def load_packed(b):
+            nc.sync.dma_start(
+                out=w2_codes[:].bitcast(I32)[:, b * BLOCK // 2 : (b + 1) * BLOCK // 2],
+                in_=w2_dram[:, b * BLOCK // 2 : (b + 1) * BLOCK // 2],
+            )
+            nc.sync.dma_start(
+                out=w3_codes[:].bitcast(I32)[:, b * BLOCK : (b + 1) * BLOCK],
+                in_=w3_dram[:, b * BLOCK : (b + 1) * BLOCK],
+            )
+
+        def entries(lst, lo, hi):
+            return lst[:, lo // PER_COL : hi // PER_COL]
+
+        nc.vector.memset(table_scales[:].bitcast(I32), 0)
+        nc.vector.memset(warm[:], 0.0)
+        nc.scalar.activation(out=warm[:, 4:5], in_=warm[:, 0:1], func=ACT.Tanh)
+        nc.sync.dma_start(list1[:], offs)
+        load_planes(nc.sync, w2_planes, w2_scales)
+        nc.sync.dma_start(list2[:], offs2)
+        nc.sync.dma_start(list3[:], offs3)
+        load_rows(("w1", 0), w1[:, :BLOCK], 0)
+        nc.sync.dma_start(out=gain_sb[:], in_=gain.rearrange("(b p t) -> p b t", b=2, t=PACK))
+        load_planes(nc.sync, table_scales, tab_scales)
+        table_words = slot_tile(3, [P, T], U32, "table_words")
+        nc.sync.dma_start(
+            out=table_words[:].bitcast(I32), in_=tab_words[0].rearrange("p t i -> p (t i)").bitcast(I32)
+        )
+
+        make_identity(nc, ident[:])
+        round_rows(("w1", 0), 2)
+        quantise(w1_codes, w1_planes, 0, grouped[("w1", 0)], BLOCK)
+
+        w2_codes = slot_tile(0, [P, 2 * H], U8, "w2_codes")
+        w3_codes = slot_tile(0.5, [P, H], U32, "w3_codes")
+        w3_planes = slot_tile(1.5, [P, H], U8, "w3_planes")
+        load_packed(0)
+        load_planes(nc.sync, w3_planes, w3_scales)
+        load_packed(1)
+        wgs_sb = slot_tile(2, [P, S], F32, "wgs_sb")
+        nc.sync.dma_start(out=wgs_sb[:], in_=wgs)
+
+        for i in range(2):
+            picked = entries(list1, i * BANK, (i + 1) * BANK)
+            nc.vector.tensor_copy(v_scales[i][:], table_scales[:].indirect(picked))
+            nc.vector.tensor_copy(v_words[i][:], table_words[:].indirect(picked))
+        for t in range(PACK):
+            nc.vector.memset(pages[t][:, :T2], 0.0)
+            nc.vector.memset(pages[t][:, T2:], -1.0)
+        load_rows(("w1", 1), w1[:, BLOCK:], 3)
+        wgt_sb = slot_tile(5, [P, M], F32, "wgt_sb")
+        nc.sync.dma_start(out=wgt_sb[:], in_=wgt)
+
+        parts = {}
+
+        def front(k, page=None):
+            b, jt = divmod(k, 8)
+            half, j0 = divmod(jt * P, BANK)
+            stat = dict(lhsT=v_words[half][:, j0 : j0 + P].bitcast(FP8X4), lhsT_scale=v_scales[half][:, j0 : j0 + P])
+            cols = slice(b * BLOCK, (b + 1) * BLOCK)
+            sum_a = psum.tile([P, BANK], F32, name="sum_a", tag="A", bufs=1)
+            sum_b = psum.tile([P, BANK], F32, name="sum_b", tag="B", bufs=2)
+            sum_c = psum.tile([P, BANK], F32, name="sum_c", tag="C", bufs=1)
+            nc.tensor.matmul_mx(out=sum_a[:], rhs=w1_codes[:, cols].bitcast(FP8X4), rhs_scale=w1_planes[:, cols],
+                                start=True, stop=True, **stat)
+            nc.tensor.matmul_mx(out=sum_b[:], rhs=w2_codes[:, 2 * b * BLOCK : 2 * (b + 1) * BLOCK].bitcast(FP4X4),
+                                rhs_scale=w2_planes[:, cols], start=True, stop=True, **stat)
+            nc.tensor.matmul_mx(out=sum_c[:], rhs=w3_codes[:, cols].bitcast(FP8X4), rhs_scale=w3_planes[:, cols],
+                                start=True, stop=True, **stat)
+            neg_a = ring.tile([P, PACK, P], F32, name="neg_a")
+            abs_c = ring.tile([P, PACK, P], F32, name="abs_c")
+            neg_max = ring.tile([P, PACK, P], F32, name="neg_max")
+            nc.scalar.activation(out=neg_a[:], in_=sum_a[:].rearrange("j (p t) -> j t p", t=PACK), func=ACT.Copy, scale=-1.0)
+            nc.scalar.activation(out=abs_c[:], in_=sum_c[:].rearrange("j (p t) -> j t p", t=PACK), func=ACT.Abs)
+            nc.vector.scalar_tensor_tensor(
+                out=neg_max[:], in0=sum_b[:].rearrange("j (p t) -> j t p", t=PACK), in1=neg_a[:],
+                scalar=-1.0 if page is None else pages[page][:, T2 : T2 + 1],
+                op0=ALU.mult, op1=ALU.min,
+            )
+            parts[k] = (abs_c, neg_max)
+
+        def back(k):
+            b, jt = divmod(k, 8)
+            abs_c, neg_max = parts[k]
+            neg_h = psum.tile([P, PACK, P], F32, name="neg_h", tag="H", bufs=2)
+            for t in range(PACK):
+                nc.tensor.matmul(neg_h[:, t, :], abs_c[:, t, :], ident[:], start=True, stop=False, is_transpose=True)
+                nc.tensor.matmul(neg_h[:, t, :], neg_max[:, t, :], ident[:], start=False, stop=True, is_transpose=True)
+            nc.scalar.activation(out=h_rows[b][:, :, jt * P : (jt + 1) * P], in_=neg_h[:], func=ACT.Copy, scale=-1.0)
+
+        def scatter(b, t, lo, hi, page):
+            nc.vector.tensor_tensor(
+                pages[page][:].indirect(entries(list2, lo, hi)), h_rows[b][:, t, lo:hi], wgs_sb[:, lo:hi], ALU.mult
+            )
+
+        wear_sb = {}
+        scaled = {}
+        readings = {}
+        tanhs = {}
+        wear_rows = wear.rearrange("(b p t) m -> b t p m", b=2, t=PACK)
+
+        def load_wear(b, t):
+            wear_sb[b, t] = slot_tile((0, 1, 7, 6)[t], [P, M], F32, "wear%d%d" % (b, t))
+            nc.sync.dma_start(out=wear_sb[b, t][:], in_=wear_rows[b, t])
+
+        def read(b, t, lo, hi, page, gain_on_vector, behind=None):
+            if lo == 0:
+                scaled[b, t] = slot_tile(8 + t, [P, M], F32, "scaled%d%d" % (b, t))
+                readings[b, t] = ring.tile([P, M], F32, name="x", tag="x", bufs=2)
+                if behind is None:
+                    tanhs[b, t] = ring.tile([P, M], F32, name="bounded", tag="bounded", bufs=2)
+                else:
+                    tanhs[b, t] = slot_tile(8 + behind, [P, M], F32, "bounded%d%d" % (b, t))
+            x = readings[b, t][:, lo:hi]
+            bounded = tanhs[b, t][:, lo:hi]
+            nc.vector.tensor_tensor(x[:], pages[page][:].indirect(entries(list3, lo, hi)), wgt_sb[:, lo:hi], ALU.mult)
+            nc.scalar.activation(out=bounded[:], in_=x[:], func=ACT.Tanh)
+            if gain_on_vector:
+                nc.vector.tensor_scalar(
+                    out=scaled[b, t][:, lo:hi], in0=bounded[:], scalar1=gain_sb[:, b, t : t + 1], scalar2=None, op0=ALU.mult
+                )
+            else:
+                nc.scalar.activation(out=scaled[b, t][:, lo:hi], in_=bounded[:], func=ACT.Copy, scale=gain_sb[:, b, t : t + 1])
+
+        turned = {}
+
+        def add_wear(b, u, c):
+            z_sum = bank([P, 2, 2, P], ("BBAC", "HHBB", "ACHH", "BBAC")[2 * b + u][c], "z_sum")
+            terms = [(source, e, mt) for source in (wear_sb, scaled) for e in range(2) for mt in range(2)]
+            for n, (source, e, mt) in enumerate(terms):
+                cols = slice(c * CHUNK + mt * P, c * CHUNK + (mt + 1) * P)
+                nc.tensor.matmul(z_sum[:, mt, e, :], source[b, 2 * u + e][:, cols], ident[:],
+                                 start=(n == 0), stop=(n == len(terms) - 1), is_transpose=True)
+            turned[b, u, c] = ring.tile([P, BANK], BF16, name="turned", tag="turned", bufs=8)
+            nc.scalar.copy(
+                turned[b, u, c][:].rearrange("m (mt p e) -> m mt p e", mt=2, e=2),
+                z_sum[:].rearrange("m mt e p -> m mt p e"),
+            )
+
+        z_values = {}
+
+        def turn_back(b, c, copy):
+            pairs = psum.tile([P, 2, CHUNK], F32, name="pairs", tag="Z", bufs=2)
+            for u in range(2):
+                words = turned[b, u, c][:].bitcast(F32)
+                for mt in range(2):
+                    nc.tensor.transpose(pairs[:, u, mt * P : (mt + 1) * P], words[:, mt * P : (mt + 1) * P], ident[:])
+            z_values[b, c] = ring.tile([P, PACK * CHUNK], BF16, name="z_values", tag="z_values", bufs=4, align_bytes=64)
+            copy(
+                z_values[b, c][:].bitcast(F32).rearrange("p (m u) -> p m u", u=2),
+                pairs[:].rearrange("p u m -> p m u"),
+            )
+
+        def quantise_z(b, c):
+            quantise(z_codes, z_planes, b * M + c * CHUNK, z_values[b, c], CHUNK)
+
+        scores = {}
+        out_rows = out.rearrange("(nt p) m -> p nt m", p=P)
+
+        def score_pass(b, c):
+            if b == 0:
+                wide = bank([P, 2, CHUNK], "HBAH"[c], "wide")
+                last = bank([P, CHUNK], "HBCH"[c], "last")
+                scores[c] = (wide, last)
+            wide, last = scores[c]
+            cols = slice(b * M + c * CHUNK, b * M + (c + 1) * CHUNK)
+            for nt in range(N // P):
+                w_cols = slice(b * N + nt * P, b * N + (nt + 1) * P)
+                nc.tensor.matmul_mx(
+                    out=wide[:, nt, :] if nt < 2 else last[:], lhsT=w4_codes[:, w_cols].bitcast(FP8X4), lhsT_scale=w4_planes[:, w_cols],
+                    rhs=z_codes[:, cols].bitcast(FP8X4), rhs_scale=z_planes[:, cols],
+                    start=(b == 0 and nt != 1), stop=(b == 1 and nt != 0),
+                )
+
+        def store(c):
+            staged = ring.tile([P, N // P, CHUNK], F32, name="staged")
+            nc.vector.tensor_copy(staged[:, 0:2, :], scores[c][0][:])
+            nc.scalar.copy(staged[:, 2, :], scores[c][1][:])
+            nc.sync.dma_start(out=out_rows[:, :, c * CHUNK : (c + 1) * CHUNK], in_=staged[:])
+
+        chunks = range(M // CHUNK)
+        front(0)
+        front(1)
+        back(0)
+        back(1)
+        front(2)
+        for t in range(PACK):
+            scatter(0, t, 0, 2 * P, t)
+            front(3 + t, (t + 1) % PACK)
+            back(2 + t)
+            if t == 2:
+                round_rows(("w1", 1), 6)
+                load_rows(("w4", 0), w4[:BLOCK, :], 3)
+        scatter(0, 0, 2 * P, BANK, 0)
+        front(7, 1)
+        back(6)
+        quantise(w1_codes, w1_planes, BLOCK, grouped[("w1", 1)], BLOCK)
+        back(7)
+        for t in range(1, PACK):
+            scatter(0, t, 2 * P, BANK, t)
+        for t in range(PACK):
+            scatter(0, t, BANK, S, t)
+            front(8 + 2 * t)
+            if t > 0:
+                back(7 + 2 * t)
+            front(9 + 2 * t, (t + 1) % PACK)
+            back(8 + 2 * t)
+            if t < 3:
+                read(0, t, 0, M, t, False)
+        back(15)
+        for t in range(PACK):
+            load_wear(0, t)
+        read(0, 3, 0, M, 3, False)
+        round_rows(("w4", 0), 12)
+        load_rows(("w4", 1), w4[BLOCK:, :], 3)
+        round_rows(("w4", 1), 13)
+        scatter(1, 0, 0, BANK, 0)
+        scatter(1, 1, 0, S, 1)
+        scatter(1, 0, BANK, S, 0)
+        for b in range(2):
+            quantise(w4_codes, w4_planes, b * N, grouped[("w4", b)], CHUNK)
+        for c in chunks:
+            add_wear(0, 0, c)
+        load_wear(1, 0)
+        load_wear(1, 1)
+        for c in chunks:
+            add_wear(0, 1, c)
+            turn_back(0, c, nc.scalar.copy)
+        load_wear(1, 2)
+        load_wear(1, 3)
+        read(1, 1, 0, M, 1, False, 3)
+        scatter(1, 2, 0, S, 1)
+        for c in chunks:
+            quantise_z(0, c)
+        read(1, 0, 0, M, 0, False, 2)
+        for c in chunks:
+            add_wear(1, 0, c)
+        read(1, 2, 0, M, 1, False, 1)
+        score_pass(0, 0)
+        scatter(1, 3, 0, S, 1)
+        for c in chunks:
+            read(1, 3, c * CHUNK, (c + 1) * CHUNK, 1, False, 1)
+            add_wear(1, 1, c)
+        for c in chunks:
+            turn_back(1, c, nc.scalar.copy if c == 0 else nc.vector.tensor_copy)
+            quantise_z(1, c)
+            if c >= 1:
+                score_pass(0, c)
+            score_pass(1, c)
+            store(c)

@@ -23,7 +23,6 @@ BLOCK = P * PACK
 BANK = 512
 CHUNK = 256
 PER_COL = 16
-SPARE = 8
 SLOT = 4096
 
 
@@ -39,29 +38,25 @@ def tile_list_banknote_pocket_scores_kernel(
         psum = ctx.enter_context(tc.psum_pool(name="psum", bufs=1))
 
         def slot_tile(slot, shape, dtype, name):
-            return shared.tile(shape, dtype, name=name, offset=int(slot * SLOT), align_bytes=64)
+            return shared.tile(shape, dtype, name=name, offset=int(slot * SLOT) // 64 * 64, align_bytes=64)
 
         def bank(shape, tag, name):
-            return psum.tile(shape, F32, name=name, tag=tag, bufs=1 if tag in "AC" else 2)
+            return psum.tile(shape, F32, name=name, tag=tag, bufs=1 if tag in "BC" else 2)
 
         list1 = keep.tile([P, S // PER_COL], U16, name="list1")
         list2 = keep.tile([P, S // PER_COL], U16, name="list2")
         list3 = keep.tile([P, M // PER_COL], U16, name="list3")
-        table_scales = keep.tile([P, T], U8, name="table_scales", align_bytes=64)
-        w1_codes = slot_tile(7, [P, H], U32, "w1_codes")
+        table_scales = slot_tile(13, [P, T], U8, "table_scales")
+        w1_codes = slot_tile(14, [P, H], U32, "w1_codes")
         w1_planes = keep.tile([P, H], U8, name="w1_planes", align_bytes=64)
         w2_planes = keep.tile([P, H], U8, name="w2_planes", align_bytes=64)
         w4_codes = keep.tile([P, 2 * N], U32, name="w4_codes", align_bytes=64)
         w4_planes = keep.tile([P, 2 * N], U8, name="w4_planes", align_bytes=64)
         z_codes = keep.tile([P, 2 * M], U32, name="z_codes", align_bytes=64)
         z_planes = keep.tile([P, 2 * M], U8, name="z_planes", align_bytes=64)
-        gain_sb = keep.tile([P, 2, PACK], F32, name="gain_sb")
         ident = keep.tile([P, P], F32, name="ident")
-        warm = slot_tile(3, [P, 8], F32, "warm")
-        pages = [keep.tile([P, T2 + SPARE], F32, name="page%d" % t) for t in range(PACK)]
-        v_words = [keep.tile([P, BANK], U32, name="v_words%d" % i, align_bytes=64) for i in range(2)]
-        v_scales = [keep.tile([P, BANK], U8, name="v_scales%d" % i, align_bytes=64) for i in range(2)]
-        h_rows = [keep.tile([P, PACK, S], F32, name="h_rows%d" % b) for b in range(2)]
+        pages = [keep.tile([P, T2], F32, name="page%d" % t) for t in range(2)]
+        h_rows = [slot_tile(20 + 4 * b, [P, PACK, S], F32, "h_rows%d" % b) for b in range(2)]
 
         def load_planes(queue, tile, src):
             for q in range(4):
@@ -78,10 +73,10 @@ def tile_list_banknote_pocket_scores_kernel(
 
         grouped = {}
 
-        def round_rows(key, slot):
+        def round_rows(key, slot, copy=nc.scalar.copy):
             width = raw[key].shape[2]
             grouped[key] = slot_tile(slot, [P, width * PACK], BF16, "grouped_%s%d" % key)
-            nc.scalar.copy(
+            copy(
                 grouped[key][:].rearrange("p (c e i) -> p c i e", e=4, i=PACK),
                 raw[key][:].rearrange("p i (c e) -> p c i e", e=4),
             )
@@ -113,69 +108,86 @@ def tile_list_banknote_pocket_scores_kernel(
         def entries(lst, lo, hi):
             return lst[:, lo // PER_COL : hi // PER_COL]
 
-        nc.vector.memset(table_scales[:].bitcast(I32), 0)
-        nc.vector.memset(warm[:], 0.0)
-        nc.scalar.activation(out=warm[:, 4:5], in_=warm[:, 0:1], func=ACT.Tanh)
+        nc.gpsimd.memset(table_scales[:].bitcast(I32), 0)
+        warm = slot_tile(0, [P, SLOT], F32, "warm")
+        nc.gpsimd.memset(warm[:, 0:8], 0.0)
+        make_identity(nc, ident[:])
+        nc.gpsimd.memset(pages[0][:], 0.0)
+        nc.gpsimd.memset(pages[1][:], 0.0)
         nc.sync.dma_start(list1[:], offs)
         load_planes(nc.sync, w2_planes, w2_scales)
         nc.sync.dma_start(list2[:], offs2)
         nc.sync.dma_start(list3[:], offs3)
-        load_rows(("w1", 0), w1[:, :BLOCK], 0)
-        nc.sync.dma_start(out=gain_sb[:], in_=gain.rearrange("(b p t) -> p b t", b=2, t=PACK))
-        load_planes(nc.sync, table_scales, tab_scales)
-        table_words = slot_tile(3, [P, T], U32, "table_words")
+        table_words = slot_tile(8, [P, T], U32, "table_words")
         nc.sync.dma_start(
             out=table_words[:].bitcast(I32), in_=tab_words[0].rearrange("p t i -> p (t i)").bitcast(I32)
         )
-
-        make_identity(nc, ident[:])
-        round_rows(("w1", 0), 2)
-        quantise(w1_codes, w1_planes, 0, grouped[("w1", 0)], BLOCK)
+        load_planes(nc.scalar, table_scales, tab_scales)
+        nc.scalar.activation(out=warm[:, 8:9], in_=warm[:, 0:1], func=ACT.Tanh)
 
         w2_codes = slot_tile(0, [P, 2 * H], U8, "w2_codes")
         w3_codes = slot_tile(0.5, [P, H], U32, "w3_codes")
         w3_planes = slot_tile(1.5, [P, H], U8, "w3_planes")
         load_packed(0)
+        load_rows(("w1", 0), w1[:, :CHUNK], 2)
+        load_rows(("w1", 1), w1[:, CHUNK:BLOCK], 3)
         load_planes(nc.sync, w3_planes, w3_scales)
         load_packed(1)
-        wgs_sb = slot_tile(2, [P, S], F32, "wgs_sb")
-        nc.sync.dma_start(out=wgs_sb[:], in_=wgs)
 
-        for i in range(2):
+        round_rows(("w1", 0), 4)
+        round_rows(("w1", 1), 28.5, nc.vector.tensor_copy)
+        for c in range(2):
+            quantise(w1_codes, w1_planes, c * CHUNK, grouped[("w1", c)], CHUNK)
+
+        v_words, v_scales = [], []
+
+        def look_up(i, slot, word_slot):
             picked = entries(list1, i * BANK, (i + 1) * BANK)
+            v_scales.append(slot_tile(slot, [P, BANK], U8, "v_scales%d" % i))
+            v_words.append(slot_tile(word_slot, [P, BANK], U32, "v_words%d" % i))
             nc.vector.tensor_copy(v_scales[i][:], table_scales[:].indirect(picked))
             nc.vector.tensor_copy(v_words[i][:], table_words[:].indirect(picked))
-        for t in range(PACK):
-            nc.vector.memset(pages[t][:, :T2], 0.0)
-            nc.vector.memset(pages[t][:, T2:], -1.0)
-        load_rows(("w1", 1), w1[:, BLOCK:], 3)
-        wgt_sb = slot_tile(5, [P, M], F32, "wgt_sb")
-        nc.sync.dma_start(out=wgt_sb[:], in_=wgt)
+
+        look_up(0, 5.25, 5.5)
+        wgs_sb = slot_tile(3, [P, S], F32, "wgs_sb")
+        gain_sb = slot_tile(4, [P, 2, PACK], F32, "gain_sb")
+        nc.sync.dma_start(out=wgs_sb[:], in_=wgs)
+        nc.sync.dma_start(out=gain_sb[:], in_=gain.rearrange("(b p t) -> p b t", b=2, t=PACK))
+        pages.append(slot_tile(28.5, [P, T2], F32, "page2"))
+        nc.gpsimd.memset(pages[2][:], 0.0)
 
         parts = {}
 
-        def front(k, page=None):
+        def front(k):
             b, jt = divmod(k, 8)
             half, j0 = divmod(jt * P, BANK)
             stat = dict(lhsT=v_words[half][:, j0 : j0 + P].bitcast(FP8X4), lhsT_scale=v_scales[half][:, j0 : j0 + P])
             cols = slice(b * BLOCK, (b + 1) * BLOCK)
-            sum_a = psum.tile([P, BANK], F32, name="sum_a", tag="A", bufs=1)
-            sum_b = psum.tile([P, BANK], F32, name="sum_b", tag="B", bufs=2)
-            sum_c = psum.tile([P, BANK], F32, name="sum_c", tag="C", bufs=1)
-            nc.tensor.matmul_mx(out=sum_a[:], rhs=w1_codes[:, cols].bitcast(FP8X4), rhs_scale=w1_planes[:, cols],
-                                start=True, stop=True, **stat)
+            sum_b = bank([P, BANK], "B", "sum_b")
+            sum_c = bank([P, BANK], "C", "sum_c")
+            sum_a = bank([P, BANK], "A", "sum_a")
             nc.tensor.matmul_mx(out=sum_b[:], rhs=w2_codes[:, 2 * b * BLOCK : 2 * (b + 1) * BLOCK].bitcast(FP4X4),
                                 rhs_scale=w2_planes[:, cols], start=True, stop=True, **stat)
             nc.tensor.matmul_mx(out=sum_c[:], rhs=w3_codes[:, cols].bitcast(FP8X4), rhs_scale=w3_planes[:, cols],
                                 start=True, stop=True, **stat)
-            neg_a = ring.tile([P, PACK, P], F32, name="neg_a")
-            abs_c = ring.tile([P, PACK, P], F32, name="abs_c")
+            nc.tensor.matmul_mx(out=sum_a[:], rhs=w1_codes[:, cols].bitcast(FP8X4), rhs_scale=w1_planes[:, cols],
+                                start=True, stop=True, **stat)
+            if k < 2:
+                neg_b = slot_tile(2 + k / 2, [P, PACK, P], F32, "neg_b%d" % k)
+            elif k in ({11: 1, 13: 2, 15: 3}):
+                neg_b = slot_tile(9 + ({11: 1, 13: 2, 15: 3})[k], [P, PACK, P], F32, "neg_b%d" % k)
+            else:
+                neg_b = ring.tile([P, PACK, P], F32, name="neg_b")
+            if k == 1 or k == 2:
+                abs_c = slot_tile(5 + k, [P, PACK, P], F32, "abs_c%d" % k)
+            else:
+                abs_c = ring.tile([P, PACK, P], F32, name="abs_c")
             neg_max = ring.tile([P, PACK, P], F32, name="neg_max")
-            nc.scalar.activation(out=neg_a[:], in_=sum_a[:].rearrange("j (p t) -> j t p", t=PACK), func=ACT.Copy, scale=-1.0)
+            nc.scalar.activation(out=neg_b[:], in_=sum_b[:].rearrange("j (p t) -> j t p", t=PACK), func=ACT.Copy, scale=-1.0)
             nc.scalar.activation(out=abs_c[:], in_=sum_c[:].rearrange("j (p t) -> j t p", t=PACK), func=ACT.Abs)
             nc.vector.scalar_tensor_tensor(
-                out=neg_max[:], in0=sum_b[:].rearrange("j (p t) -> j t p", t=PACK), in1=neg_a[:],
-                scalar=-1.0 if page is None else pages[page][:, T2 : T2 + 1],
+                out=neg_max[:], in0=sum_a[:].rearrange("j (p t) -> j t p", t=PACK), in1=neg_b[:],
+                scalar=-1.0,
                 op0=ALU.mult, op1=ALU.min,
             )
             parts[k] = (abs_c, neg_max)
@@ -189,7 +201,8 @@ def tile_list_banknote_pocket_scores_kernel(
                 nc.tensor.matmul(neg_h[:, t, :], neg_max[:, t, :], ident[:], start=False, stop=True, is_transpose=True)
             nc.scalar.activation(out=h_rows[b][:, :, jt * P : (jt + 1) * P], in_=neg_h[:], func=ACT.Copy, scale=-1.0)
 
-        def scatter(b, t, lo, hi, page):
+        def scatter(b, t, first, last, page):
+            lo, hi = first * P, last * P
             nc.vector.tensor_tensor(
                 pages[page][:].indirect(entries(list2, lo, hi)), h_rows[b][:, t, lo:hi], wgs_sb[:, lo:hi], ALU.mult
             )
@@ -201,32 +214,31 @@ def tile_list_banknote_pocket_scores_kernel(
         wear_rows = wear.rearrange("(b p t) m -> b t p m", b=2, t=PACK)
 
         def load_wear(b, t):
-            wear_sb[b, t] = slot_tile((0, 1, 7, 6)[t], [P, M], F32, "wear%d%d" % (b, t))
+            wear_sb[b, t] = slot_tile((0, 1, 14, 15)[t], [P, M], F32, "wear%d%d" % (b, t))
             nc.sync.dma_start(out=wear_sb[b, t][:], in_=wear_rows[b, t])
 
-        def read(b, t, lo, hi, page, gain_on_vector, behind=None):
+        def read(b, t, lo, hi, page, apply_gain, behind=None):
             if lo == 0:
-                scaled[b, t] = slot_tile(8 + t, [P, M], F32, "scaled%d%d" % (b, t))
-                readings[b, t] = ring.tile([P, M], F32, name="x", tag="x", bufs=2)
+                if b == 0 and t in ({11: 1, 13: 2, 15: 3}).values():
+                    readings[b, t] = slot_tile(9 + t, [P, M], F32, "x%d" % t)
+                else:
+                    readings[b, t] = ring.tile([P, M], F32, name="x", tag="x", bufs=2)
                 if behind is None:
                     tanhs[b, t] = ring.tile([P, M], F32, name="bounded", tag="bounded", bufs=2)
                 else:
-                    tanhs[b, t] = slot_tile(8 + behind, [P, M], F32, "bounded%d%d" % (b, t))
+                    tanhs[b, t] = slot_tile(16 + behind, [P, M], F32, "bounded%d%d" % (b, t))
             x = readings[b, t][:, lo:hi]
             bounded = tanhs[b, t][:, lo:hi]
             nc.vector.tensor_tensor(x[:], pages[page][:].indirect(entries(list3, lo, hi)), wgt_sb[:, lo:hi], ALU.mult)
             nc.scalar.activation(out=bounded[:], in_=x[:], func=ACT.Tanh)
-            if gain_on_vector:
-                nc.vector.tensor_scalar(
-                    out=scaled[b, t][:, lo:hi], in0=bounded[:], scalar1=gain_sb[:, b, t : t + 1], scalar2=None, op0=ALU.mult
-                )
-            else:
-                nc.scalar.activation(out=scaled[b, t][:, lo:hi], in_=bounded[:], func=ACT.Copy, scale=gain_sb[:, b, t : t + 1])
+            if apply_gain:
+                scaled[b, t] = slot_tile(16 + t, [P, M], F32, "scaled%d%d" % (b, t))
+                nc.scalar.activation(out=scaled[b, t][:], in_=bounded, func=ACT.Copy, scale=gain_sb[:, b, t : t + 1])
 
         turned = {}
 
         def add_wear(b, u, c):
-            z_sum = bank([P, 2, 2, P], ("BBAC", "HHBB", "ACHH", "BBAC")[2 * b + u][c], "z_sum")
+            z_sum = bank([P, 2, 2, P], ("AABC", "HHAA", "BCAA")[2 * b + u][c], "z_sum")
             terms = [(source, e, mt) for source in (wear_sb, scaled) for e in range(2) for mt in range(2)]
             for n, (source, e, mt) in enumerate(terms):
                 cols = slice(c * CHUNK + mt * P, c * CHUNK + (mt + 1) * P)
@@ -240,16 +252,38 @@ def tile_list_banknote_pocket_scores_kernel(
 
         z_values = {}
 
-        def turn_back(b, c, copy):
-            pairs = psum.tile([P, 2, CHUNK], F32, name="pairs", tag="Z", bufs=2)
-            for u in range(2):
-                words = turned[b, u, c][:].bitcast(F32)
-                for mt in range(2):
-                    nc.tensor.transpose(pairs[:, u, mt * P : (mt + 1) * P], words[:, mt * P : (mt + 1) * P], ident[:])
+        def interleave(b, c, pairs, copy):
             z_values[b, c] = ring.tile([P, PACK * CHUNK], BF16, name="z_values", tag="z_values", bufs=4, align_bytes=64)
             copy(
                 z_values[b, c][:].bitcast(F32).rearrange("p (m u) -> p m u", u=2),
                 pairs[:].rearrange("p u m -> p m u"),
+            )
+
+        def turn_pair(target, b, u, c):
+            words = turned[b, u, c][:].bitcast(F32)
+            for mt in range(2):
+                nc.tensor.transpose(target[:, mt * P : (mt + 1) * P], words[:, mt * P : (mt + 1) * P], ident[:])
+
+        def turn_back(b, c):
+            pairs = bank([P, 2, CHUNK], "Z", "pairs")
+            for u in range(2):
+                turn_pair(pairs[:, u, :], b, u, c)
+            interleave(b, c, pairs, nc.scalar.copy)
+
+        last_pairs = {}
+
+        def turn_back_first_pair(c):
+            pair = bank([P, CHUNK], "HHZZ"[c], "pair")
+            turn_pair(pair, 1, 0, c)
+            last_pairs[c] = ring.tile([P, 2, CHUNK], F32, name="last_pairs", tag="last_pairs", bufs=4)
+            nc.scalar.copy(last_pairs[c][:, 0, :], pair[:])
+
+        def finish_direct(t, c):
+            cols = slice(c * CHUNK, (c + 1) * CHUNK)
+            halves = last_pairs[c][:, 1, :].bitcast(BF16).rearrange("p (m e) -> p m e", e=2)
+            nc.vector.scalar_tensor_tensor(
+                out=halves[:, :, t - 2], in0=tanhs[1, t][:, cols], scalar=gain_sb[:, 1, t : t + 1],
+                in1=wear_sb[1, t][:, cols], op0=ALU.mult, op1=ALU.add,
             )
 
         def quantise_z(b, c):
@@ -260,8 +294,8 @@ def tile_list_banknote_pocket_scores_kernel(
 
         def score_pass(b, c):
             if b == 0:
-                wide = bank([P, 2, CHUNK], "HBAH"[c], "wide")
-                last = bank([P, CHUNK], "HBCH"[c], "last")
+                wide = bank([P, 2, CHUNK], "BCAA"[c], "wide")
+                last = bank([P, CHUNK], "HHZZ"[c], "last")
                 scores[c] = (wide, last)
             wide, last = scores[c]
             cols = slice(b * M + c * CHUNK, b * M + (c + 1) * CHUNK)
@@ -273,51 +307,56 @@ def tile_list_banknote_pocket_scores_kernel(
                     start=(b == 0 and nt != 1), stop=(b == 1 and nt != 0),
                 )
 
-        def store(c):
-            staged = ring.tile([P, N // P, CHUNK], F32, name="staged")
-            nc.vector.tensor_copy(staged[:, 0:2, :], scores[c][0][:])
-            nc.scalar.copy(staged[:, 2, :], scores[c][1][:])
+        def store(c, copy_wide, copy_last):
+            staged = ring.tile([P, N // P, CHUNK], F32, name="staged", bufs=4)
+            copy_wide(staged[:, 0:2, :], scores[c][0][:])
+            copy_last(staged[:, 2, :], scores[c][1][:])
             nc.sync.dma_start(out=out_rows[:, :, c * CHUNK : (c + 1) * CHUNK], in_=staged[:])
 
         chunks = range(M // CHUNK)
+        reads = {9: 0, 11: 1, 13: 2, 15: 3}
+        put_up_to = {}
+
+        def put(k, t):
+            b, jt = divmod(k, 8)
+            scatter(b, t, put_up_to.get((b, t), 0), jt + 1, t)
+            put_up_to[b, t] = jt + 1
+
         front(0)
-        front(1)
-        back(0)
-        back(1)
-        front(2)
-        for t in range(PACK):
-            scatter(0, t, 0, 2 * P, t)
-            front(3 + t, (t + 1) % PACK)
-            back(2 + t)
-            if t == 2:
-                round_rows(("w1", 1), 6)
-                load_rows(("w4", 0), w4[:BLOCK, :], 3)
-        scatter(0, 0, 2 * P, BANK, 0)
-        front(7, 1)
-        back(6)
-        quantise(w1_codes, w1_planes, BLOCK, grouped[("w1", 1)], BLOCK)
-        back(7)
-        for t in range(1, PACK):
-            scatter(0, t, 2 * P, BANK, t)
-        for t in range(PACK):
-            scatter(0, t, BANK, S, t)
-            front(8 + 2 * t)
-            if t > 0:
-                back(7 + 2 * t)
-            front(9 + 2 * t, (t + 1) % PACK)
-            back(8 + 2 * t)
-            if t < 3:
-                read(0, t, 0, M, t, False)
-        back(15)
+        for k in range(16):
+            if k < 15:
+                front(k + 1)
+            if k == 0:
+                look_up(1, 2, 2.5)
+                pages.append(slot_tile(8, [P, T2], F32, "page3"))
+                nc.gpsimd.memset(pages[3][:], 0.0)
+                wgt_sb = slot_tile(13, [P, M], F32, "wgt_sb")
+                nc.sync.dma_start(out=wgt_sb[:], in_=wgt)
+            back(k)
+            if k == 2:
+                load_rows(("w1", 2), w1[:, BLOCK : BLOCK + CHUNK], 6)
+                load_rows(("w1", 3), w1[:, BLOCK + CHUNK :], 7)
+            if k == 4 or k == 5:
+                round_rows(("w1", k - 2), 15 + (k - 4) / 2)
+                quantise(w1_codes, w1_planes, (k - 2) * CHUNK, grouped[("w1", k - 2)], CHUNK)
+            if k in reads:
+                read(0, reads[k], 0, M, reads[k], True)
+            if k == 0:
+                put(k, 0)
+            if k < 7:
+                put(k, (k + 1) % PACK)
+            if k == 7:
+                for t in range(PACK):
+                    put(k, t)
+            if k in ({10:0,11:1,12:0,13:1,14:0}):
+                put(k, ({10:0,11:1,12:0,13:1,14:0})[k])
+        put(15, 0)
+        put(15, 1)
         for t in range(PACK):
             load_wear(0, t)
-        read(0, 3, 0, M, 3, False)
-        round_rows(("w4", 0), 12)
-        load_rows(("w4", 1), w4[BLOCK:, :], 3)
-        round_rows(("w4", 1), 13)
-        scatter(1, 0, 0, BANK, 0)
-        scatter(1, 1, 0, S, 1)
-        scatter(1, 0, BANK, S, 0)
+        for b in range(2):
+            load_rows(("w4", b), w4[b * BLOCK : (b + 1) * BLOCK, :], 20 + 2 * b)
+            round_rows(("w4", b), 6 + b)
         for b in range(2):
             quantise(w4_codes, w4_planes, b * N, grouped[("w4", b)], CHUNK)
         for c in chunks:
@@ -326,26 +365,28 @@ def tile_list_banknote_pocket_scores_kernel(
         load_wear(1, 1)
         for c in chunks:
             add_wear(0, 1, c)
-            turn_back(0, c, nc.scalar.copy)
+            turn_back(0, c)
         load_wear(1, 2)
         load_wear(1, 3)
-        read(1, 1, 0, M, 1, False, 3)
-        scatter(1, 2, 0, S, 1)
+        read(1, 1, 0, M, 1, True, 3)
+        scatter(1, 2, 0, 8, 1)
         for c in chunks:
             quantise_z(0, c)
-        read(1, 0, 0, M, 0, False, 2)
+        read(1, 0, 0, M, 0, True, 2)
         for c in chunks:
             add_wear(1, 0, c)
         read(1, 2, 0, M, 1, False, 1)
-        score_pass(0, 0)
-        scatter(1, 3, 0, S, 1)
         for c in chunks:
-            read(1, 3, c * CHUNK, (c + 1) * CHUNK, 1, False, 1)
-            add_wear(1, 1, c)
+            turn_back_first_pair(c)
         for c in chunks:
-            turn_back(1, c, nc.scalar.copy if c == 0 else nc.vector.tensor_copy)
+            score_pass(0, c)
+        scatter(1, 3, 0, 8, 1)
+        for c in chunks:
+            read(1, 3, c * CHUNK, (c + 1) * CHUNK, 1, False, 0)
+        for c in chunks:
+            finish_direct(2, c)
+            finish_direct(3, c)
+            interleave(1, c, last_pairs[c], nc.scalar.copy)
             quantise_z(1, c)
-            if c >= 1:
-                score_pass(0, c)
             score_pass(1, c)
-            store(c)
+            store(c, nc.scalar.copy, nc.vector.tensor_copy)

@@ -56,7 +56,6 @@ def tile_list_banknote_pocket_scores_kernel(
         z_planes = keep.tile([P, 2 * M], U8, name="z_planes", align_bytes=64)
         ident = keep.tile([P, P], F32, name="ident")
         pages = [keep.tile([P, T2], F32, name="page%d" % t) for t in range(2)]
-        h_rows = [slot_tile(20 + 4 * b, [P, PACK, S], F32, "h_rows%d" % b) for b in range(2)]
 
         def load_planes(queue, tile, src):
             for q in range(4):
@@ -71,13 +70,9 @@ def tile_list_banknote_pocket_scores_kernel(
             raw[key] = slot_tile(slot, [P, PACK, width], F32, "raw_%s%d" % key)
             nc.sync.dma_start(out=raw[key][:], in_=rows.rearrange("(p i) w -> p i w", i=PACK))
 
-        grouped = {}
-
-        def round_rows(key, slot, copy=nc.scalar.copy):
-            width = raw[key].shape[2]
-            grouped[key] = slot_tile(slot, [P, width * PACK], BF16, "grouped_%s%d" % key)
+        def round_rows(key, target, copy=nc.scalar.copy):
             copy(
-                grouped[key][:].rearrange("p (c e i) -> p c i e", e=4, i=PACK),
+                target.rearrange("p (c e i) -> p c i e", e=4, i=PACK),
                 raw[key][:].rearrange("p i (c e) -> p c i e", e=4),
             )
 
@@ -95,15 +90,10 @@ def tile_list_banknote_pocket_scores_kernel(
         w2_dram = w2_words[0].bitcast(I32)
         w3_dram = w3_words[0].rearrange("p c i -> p (c i)").bitcast(I32)
 
-        def load_packed(b):
-            nc.sync.dma_start(
-                out=w2_codes[:].bitcast(I32)[:, b * BLOCK // 2 : (b + 1) * BLOCK // 2],
-                in_=w2_dram[:, b * BLOCK // 2 : (b + 1) * BLOCK // 2],
-            )
-            nc.sync.dma_start(
-                out=w3_codes[:].bitcast(I32)[:, b * BLOCK : (b + 1) * BLOCK],
-                in_=w3_dram[:, b * BLOCK : (b + 1) * BLOCK],
-            )
+        def load_words(codes, dram, b):
+            width = dram.shape[1] // 2
+            cols = slice(b * width, (b + 1) * width)
+            nc.sync.dma_start(out=codes[:].bitcast(I32)[:, cols], in_=dram[:, cols])
 
         def entries(lst, lo, hi):
             return lst[:, lo // PER_COL : hi // PER_COL]
@@ -112,10 +102,10 @@ def tile_list_banknote_pocket_scores_kernel(
         warm = slot_tile(0, [P, SLOT], F32, "warm")
         nc.gpsimd.memset(warm[:, 0:8], 0.0)
         make_identity(nc, ident[:])
+        load_planes(nc.gpsimd, w2_planes, w2_scales)
         nc.gpsimd.memset(pages[0][:], 0.0)
         nc.gpsimd.memset(pages[1][:], 0.0)
         nc.sync.dma_start(list1[:], offs)
-        load_planes(nc.sync, w2_planes, w2_scales)
         nc.sync.dma_start(list2[:], offs2)
         nc.sync.dma_start(list3[:], offs3)
         table_words = slot_tile(8, [P, T], U32, "table_words")
@@ -128,16 +118,19 @@ def tile_list_banknote_pocket_scores_kernel(
         w2_codes = slot_tile(0, [P, 2 * H], U8, "w2_codes")
         w3_codes = slot_tile(0.5, [P, H], U32, "w3_codes")
         w3_planes = slot_tile(1.5, [P, H], U8, "w3_planes")
-        load_packed(0)
+        load_words(w2_codes, w2_dram, 0)
         load_rows(("w1", 0), w1[:, :CHUNK], 2)
         load_rows(("w1", 1), w1[:, CHUNK:BLOCK], 3)
+        load_words(w3_codes, w3_dram, 0)
         load_planes(nc.sync, w3_planes, w3_scales)
-        load_packed(1)
+        load_words(w2_codes, w2_dram, 1)
+        load_words(w3_codes, w3_dram, 1)
 
-        round_rows(("w1", 0), 4)
-        round_rows(("w1", 1), 28.5, nc.vector.tensor_copy)
+        first = [slot_tile(slot, [P, PACK * CHUNK], BF16, "w1_values%d" % c) for c, slot in enumerate((4, 28.75))]
+        round_rows(("w1", 0), first[0][:])
+        round_rows(("w1", 1), first[1][:], nc.vector.tensor_copy)
         for c in range(2):
-            quantise(w1_codes, w1_planes, c * CHUNK, grouped[("w1", c)], CHUNK)
+            quantise(w1_codes, w1_planes, c * CHUNK, first[c], CHUNK)
 
         v_words, v_scales = [], []
 
@@ -153,9 +146,12 @@ def tile_list_banknote_pocket_scores_kernel(
         gain_sb = slot_tile(4, [P, 2, PACK], F32, "gain_sb")
         nc.sync.dma_start(out=wgs_sb[:], in_=wgs)
         nc.sync.dma_start(out=gain_sb[:], in_=gain.rearrange("(b p t) -> p b t", b=2, t=PACK))
-        pages.append(slot_tile(28.5, [P, T2], F32, "page2"))
+        pages.append(slot_tile(27, [P, T2], F32, "page2"))
+        pages.append(slot_tile(29, [P, T2], F32, "page3"))
         nc.gpsimd.memset(pages[2][:], 0.0)
+        nc.gpsimd.memset(pages[3][:], 0.0)
 
+        h_rows = [slot_tile((20, 8)[b], [P, PACK, S], F32, "h_rows%d" % b) for b in range(2)]
         parts = {}
 
         def front(k):
@@ -163,8 +159,8 @@ def tile_list_banknote_pocket_scores_kernel(
             half, j0 = divmod(jt * P, BANK)
             stat = dict(lhsT=v_words[half][:, j0 : j0 + P].bitcast(FP8X4), lhsT_scale=v_scales[half][:, j0 : j0 + P])
             cols = slice(b * BLOCK, (b + 1) * BLOCK)
-            sum_b = bank([P, BANK], "B", "sum_b")
-            sum_c = bank([P, BANK], "C", "sum_c")
+            sum_b = bank([P, BANK], "BZ"[k % 2], "sum_b")
+            sum_c = bank([P, BANK], "CZ"[k % 2], "sum_c")
             sum_a = bank([P, BANK], "A", "sum_a")
             nc.tensor.matmul_mx(out=sum_b[:], rhs=w2_codes[:, 2 * b * BLOCK : 2 * (b + 1) * BLOCK].bitcast(FP4X4),
                                 rhs_scale=w2_planes[:, cols], start=True, stop=True, **stat)
@@ -175,7 +171,7 @@ def tile_list_banknote_pocket_scores_kernel(
             if k < 2:
                 neg_b = slot_tile(2 + k / 2, [P, PACK, P], F32, "neg_b%d" % k)
             elif k in ({11: 1, 13: 2, 15: 3}):
-                neg_b = slot_tile(9 + ({11: 1, 13: 2, 15: 3})[k], [P, PACK, P], F32, "neg_b%d" % k)
+                neg_b = slot_tile(23 + ({11: 1, 13: 2, 15: 3})[k], [P, PACK, P], F32, "neg_b%d" % k)
             else:
                 neg_b = ring.tile([P, PACK, P], F32, name="neg_b")
             if k == 1 or k == 2:
@@ -197,8 +193,9 @@ def tile_list_banknote_pocket_scores_kernel(
             abs_c, neg_max = parts[k]
             neg_h = psum.tile([P, PACK, P], F32, name="neg_h", tag="H", bufs=2)
             for t in range(PACK):
-                nc.tensor.matmul(neg_h[:, t, :], abs_c[:, t, :], ident[:], start=True, stop=False, is_transpose=True)
-                nc.tensor.matmul(neg_h[:, t, :], neg_max[:, t, :], ident[:], start=False, stop=True, is_transpose=True)
+                nc.tensor.matmul(neg_h[:, t, :], abs_c[:, t, :], ident[:], start=(t == 0), stop=False, is_transpose=True)
+            for t in range(PACK):
+                nc.tensor.matmul(neg_h[:, t, :], neg_max[:, t, :], ident[:], start=False, stop=(t == PACK - 1), is_transpose=True)
             nc.scalar.activation(out=h_rows[b][:, :, jt * P : (jt + 1) * P], in_=neg_h[:], func=ACT.Copy, scale=-1.0)
 
         def scatter(b, t, first, last, page):
@@ -220,7 +217,7 @@ def tile_list_banknote_pocket_scores_kernel(
         def read(b, t, lo, hi, page, apply_gain, behind=None):
             if lo == 0:
                 if b == 0 and t in ({11: 1, 13: 2, 15: 3}).values():
-                    readings[b, t] = slot_tile(9 + t, [P, M], F32, "x%d" % t)
+                    readings[b, t] = slot_tile(23 + t, [P, M], F32, "x%d" % t)
                 else:
                     readings[b, t] = ring.tile([P, M], F32, name="x", tag="x", bufs=2)
                 if behind is None:
@@ -250,14 +247,8 @@ def tile_list_banknote_pocket_scores_kernel(
                 z_sum[:].rearrange("m mt e p -> m mt p e"),
             )
 
-        z_values = {}
-
-        def interleave(b, c, pairs, copy):
-            z_values[b, c] = ring.tile([P, PACK * CHUNK], BF16, name="z_values", tag="z_values", bufs=4, align_bytes=64)
-            copy(
-                z_values[b, c][:].bitcast(F32).rearrange("p (m u) -> p m u", u=2),
-                pairs[:].rearrange("p u m -> p m u"),
-            )
+        def interleave(values, pairs):
+            nc.scalar.copy(values.bitcast(F32).rearrange("p (m u) -> p m u", u=2), pairs[:].rearrange("p u m -> p m u"))
 
         def turn_pair(target, b, u, c):
             words = turned[b, u, c][:].bitcast(F32)
@@ -268,50 +259,52 @@ def tile_list_banknote_pocket_scores_kernel(
             pairs = bank([P, 2, CHUNK], "Z", "pairs")
             for u in range(2):
                 turn_pair(pairs[:, u, :], b, u, c)
-            interleave(b, c, pairs, nc.scalar.copy)
+            interleave(z_first[:, c * PACK * CHUNK : (c + 1) * PACK * CHUNK], pairs)
 
+        pieces = [(0,256),(256,512),(512,768),(768,1024)]
         last_pairs = {}
 
         def turn_back_first_pair(c):
             pair = bank([P, CHUNK], "HHZZ"[c], "pair")
             turn_pair(pair, 1, 0, c)
-            last_pairs[c] = ring.tile([P, 2, CHUNK], F32, name="last_pairs", tag="last_pairs", bufs=4)
-            nc.scalar.copy(last_pairs[c][:, 0, :], pair[:])
+            for lo, hi in pieces:
+                if lo // CHUNK == c:
+                    last_pairs[lo] = ring.tile([P, 2, hi - lo], F32, name="last_pairs", tag="last_pairs", bufs=len(pieces))
+                    nc.scalar.copy(last_pairs[lo][:, 0, :], pair[:, lo - c * CHUNK : hi - c * CHUNK])
 
-        def finish_direct(t, c):
-            cols = slice(c * CHUNK, (c + 1) * CHUNK)
-            halves = last_pairs[c][:, 1, :].bitcast(BF16).rearrange("p (m e) -> p m e", e=2)
+        def finish_direct(t, lo, hi):
+            halves = last_pairs[lo][:, 1, :].bitcast(BF16).rearrange("p (m e) -> p m e", e=2)
             nc.vector.scalar_tensor_tensor(
-                out=halves[:, :, t - 2], in0=tanhs[1, t][:, cols], scalar=gain_sb[:, 1, t : t + 1],
-                in1=wear_sb[1, t][:, cols], op0=ALU.mult, op1=ALU.add,
+                out=halves[:, :, t - 2], in0=tanhs[1, t][:, lo:hi], scalar=gain_sb[:, 1, t : t + 1],
+                in1=wear_sb[1, t][:, lo:hi], op0=ALU.mult, op1=ALU.add,
             )
-
-        def quantise_z(b, c):
-            quantise(z_codes, z_planes, b * M + c * CHUNK, z_values[b, c], CHUNK)
 
         scores = {}
         out_rows = out.rearrange("(nt p) m -> p nt m", p=P)
+        score_tags = list("BHCHAZAZ")
 
-        def score_pass(b, c):
+        def score_pass(b, lo, hi):
+            per_bank = min(N // P, BANK // (hi - lo))
             if b == 0:
-                wide = bank([P, 2, CHUNK], "BCAA"[c], "wide")
-                last = bank([P, CHUNK], "HHZZ"[c], "last")
-                scores[c] = (wide, last)
-            wide, last = scores[c]
-            cols = slice(b * M + c * CHUNK, b * M + (c + 1) * CHUNK)
-            for nt in range(N // P):
-                w_cols = slice(b * N + nt * P, b * N + (nt + 1) * P)
-                nc.tensor.matmul_mx(
-                    out=wide[:, nt, :] if nt < 2 else last[:], lhsT=w4_codes[:, w_cols].bitcast(FP8X4), lhsT_scale=w4_planes[:, w_cols],
-                    rhs=z_codes[:, cols].bitcast(FP8X4), rhs_scale=z_planes[:, cols],
-                    start=(b == 0 and nt != 1), stop=(b == 1 and nt != 0),
-                )
+                scores[lo] = []
+                for nt in range(0, N // P, per_bank):
+                    count = min(per_bank, N // P - nt)
+                    scores[lo].append((nt, count, bank([P, count, hi - lo], score_tags.pop(0), "score")))
+            cols = slice(b * M + lo, b * M + hi)
+            for first, count, sums in scores[lo]:
+                for i in range(count):
+                    w_cols = slice(b * N + (first + i) * P, b * N + (first + i + 1) * P)
+                    nc.tensor.matmul_mx(
+                        out=sums[:, i, :], lhsT=w4_codes[:, w_cols].bitcast(FP8X4), lhsT_scale=w4_planes[:, w_cols],
+                        rhs=z_codes[:, cols].bitcast(FP8X4), rhs_scale=z_planes[:, cols],
+                        start=(b == 0 and i == 0), stop=(b == 1 and i == count - 1),
+                    )
 
-        def store(c, copy_wide, copy_last):
-            staged = ring.tile([P, N // P, CHUNK], F32, name="staged", bufs=4)
-            copy_wide(staged[:, 0:2, :], scores[c][0][:])
-            copy_last(staged[:, 2, :], scores[c][1][:])
-            nc.sync.dma_start(out=out_rows[:, :, c * CHUNK : (c + 1) * CHUNK], in_=staged[:])
+        def store(lo, hi, copies):
+            staged = ring.tile([P, N // P, hi - lo], F32, name="staged", tag="staged", bufs=len(pieces))
+            for (first, count, sums), copy in zip(scores[lo], copies):
+                copy(staged[:, first : first + count, :], sums[:])
+            nc.sync.dma_start(out=out_rows[:, :, lo:hi], in_=staged[:])
 
         chunks = range(M // CHUNK)
         reads = {9: 0, 11: 1, 13: 2, 15: 3}
@@ -319,7 +312,7 @@ def tile_list_banknote_pocket_scores_kernel(
 
         def put(k, t):
             b, jt = divmod(k, 8)
-            scatter(b, t, put_up_to.get((b, t), 0), jt + 1, t)
+            scatter(b, t, put_up_to.get((b, t), 0), jt + 1, (t + 2) % PACK)
             put_up_to[b, t] = jt + 1
 
         front(0)
@@ -328,65 +321,63 @@ def tile_list_banknote_pocket_scores_kernel(
                 front(k + 1)
             if k == 0:
                 look_up(1, 2, 2.5)
-                pages.append(slot_tile(8, [P, T2], F32, "page3"))
-                nc.gpsimd.memset(pages[3][:], 0.0)
                 wgt_sb = slot_tile(13, [P, M], F32, "wgt_sb")
                 nc.sync.dma_start(out=wgt_sb[:], in_=wgt)
             back(k)
             if k == 2:
                 load_rows(("w1", 2), w1[:, BLOCK : BLOCK + CHUNK], 6)
                 load_rows(("w1", 3), w1[:, BLOCK + CHUNK :], 7)
+                second = slot_tile(15, [P, PACK * BLOCK], BF16, "w1_values2")
             if k == 4 or k == 5:
-                round_rows(("w1", k - 2), 15 + (k - 4) / 2)
-                quantise(w1_codes, w1_planes, (k - 2) * CHUNK, grouped[("w1", k - 2)], CHUNK)
+                round_rows(("w1", k - 2), second[:, (k - 4) * PACK * CHUNK : (k - 3) * PACK * CHUNK])
+            if k == 5:
+                quantise(w1_codes, w1_planes, BLOCK, second, BLOCK)
             if k in reads:
-                read(0, reads[k], 0, M, reads[k], True)
-            if k == 0:
-                put(k, 0)
-            if k < 7:
-                put(k, (k + 1) % PACK)
-            if k == 7:
-                for t in range(PACK):
+                read(0, reads[k], 0, M, (reads[k] + 2) % PACK, True)
+            if k < 8:
+                for t in ((2, 3) if k % 2 == 0 else (0, 1) if k < 7 else (0, 1, 2, 3)):
                     put(k, t)
-            if k in ({10:0,11:1,12:0,13:1,14:0}):
-                put(k, ({10:0,11:1,12:0,13:1,14:0})[k])
+            if k in ({9:0,11:1,13:0,14:1}):
+                put(k, ({9:0,11:1,13:0,14:1})[k])
         put(15, 0)
         put(15, 1)
         for t in range(PACK):
             load_wear(0, t)
+        w4_values = slot_tile(6, [P, 2 * PACK * N], BF16, "w4_values")
         for b in range(2):
             load_rows(("w4", b), w4[b * BLOCK : (b + 1) * BLOCK, :], 20 + 2 * b)
-            round_rows(("w4", b), 6 + b)
-        for b in range(2):
-            quantise(w4_codes, w4_planes, b * N, grouped[("w4", b)], CHUNK)
+            round_rows(("w4", b), w4_values[:, b * PACK * N : (b + 1) * PACK * N])
+        quantise(w4_codes, w4_planes, 0, w4_values, BLOCK)
         for c in chunks:
             add_wear(0, 0, c)
         load_wear(1, 0)
         load_wear(1, 1)
+        z_first = slot_tile(24, [P, PACK * M], BF16, "z_first")
         for c in chunks:
             add_wear(0, 1, c)
             turn_back(0, c)
         load_wear(1, 2)
         load_wear(1, 3)
-        read(1, 1, 0, M, 1, True, 3)
-        scatter(1, 2, 0, 8, 1)
-        for c in chunks:
-            quantise_z(0, c)
-        read(1, 0, 0, M, 0, True, 2)
+        read(1, 1, 0, M, 3, True, 3)
+        scatter(1, 2, 0, 8, 3)
+        quantise(z_codes, z_planes, 0, z_first, M)
+        read(1, 0, 0, M, 2, True, 2)
         for c in chunks:
             add_wear(1, 0, c)
-        read(1, 2, 0, M, 1, False, 1)
+        read(1, 2, 0, M, 3, False, 1)
         for c in chunks:
             turn_back_first_pair(c)
-        for c in chunks:
-            score_pass(0, c)
-        scatter(1, 3, 0, 8, 1)
-        for c in chunks:
-            read(1, 3, c * CHUNK, (c + 1) * CHUNK, 1, False, 0)
-        for c in chunks:
-            finish_direct(2, c)
-            finish_direct(3, c)
-            interleave(1, c, last_pairs[c], nc.scalar.copy)
-            quantise_z(1, c)
-            score_pass(1, c)
-            store(c, nc.scalar.copy, nc.vector.tensor_copy)
+        for lo, hi in pieces:
+            score_pass(0, lo, hi)
+        scatter(1, 3, 0, 8, 3)
+        for lo, hi in pieces:
+            read(1, 3, lo, hi, 3, False, 0)
+        for n, (lo, hi) in enumerate(pieces):
+            for t in (3,2):
+                finish_direct(t, lo, hi)
+            values = ring.tile([P, PACK * CHUNK], BF16, name="z_values", tag="z_values", bufs=4, align_bytes=64)
+            interleave(values[:], last_pairs[lo])
+            quantise(z_codes, z_planes, M + lo, values, CHUNK)
+            score_pass(1, lo, hi)
+        for n, (lo, hi) in enumerate(pieces):
+            store(lo, hi, (nc.vector.tensor_copy, nc.scalar.copy))

from contextlib import ExitStack

import concourse.mybir as mybir
from concourse.masks import make_identity

K, H, N, T, S, M, T2 = 512, 1024, 384, 4096, 1024, 1024, 2048
FLOPS = 2 * (3 * K * H * S + H * N * M)

F32 = mybir.dt.float32
BF16 = mybir.dt.bfloat16
I32 = mybir.dt.int32
U32 = mybir.dt.uint32
U16 = mybir.dt.uint16
U8 = mybir.dt.uint8
FP8X4 = mybir.dt.float8_e4m3fn_x4
FP4X4 = mybir.dt.float4_e2m1fn_x4
ALU = mybir.AluOpType
ACT = mybir.ActivationFunctionType

P = 128
PACK = 4
BLOCK = P * PACK
BANK = 512
CHUNK = 256
PER_COL = 16
SLOT = 4096


def tile_list_banknote_pocket_scores_kernel(
    tc, tab_words, tab_scales, offs, w1, w2_words, w2_scales, w3_words, w3_scales,
    wgs, offs2, wgt, offs3, gain, wear, w4, out,
):
    nc = tc.nc
    with ExitStack() as ctx:
        keep = ctx.enter_context(tc.tile_pool(name="keep", bufs=1))
        ring = ctx.enter_context(tc.tile_pool(name="ring", bufs=2))
        shared = ctx.enter_context(tc.tile_pool(name="shared", bufs=1))
        psum = ctx.enter_context(tc.psum_pool(name="psum", bufs=1))

        def slot_tile(slot, shape, dtype, name):
            return shared.tile(shape, dtype, name=name, offset=int(slot * SLOT) // 64 * 64, align_bytes=64)

        def bank(shape, tag, name):
            return psum.tile(shape, F32, name=name, tag=tag, bufs=1 if tag in "BC" else 2)

        list1 = keep.tile([P, S // PER_COL], U16, name="list1")
        list2 = keep.tile([P, S // PER_COL], U16, name="list2")
        list3 = keep.tile([P, M // PER_COL], U16, name="list3")
        table_scales = slot_tile(13, [P, T], U8, "table_scales")
        w1_codes = slot_tile(14, [P, H], U32, "w1_codes")
        w1_planes = keep.tile([P, H], U8, name="w1_planes", align_bytes=64)
        w2_planes = keep.tile([P, H], U8, name="w2_planes", align_bytes=64)
        w4_codes = keep.tile([P, 2 * N], U32, name="w4_codes", align_bytes=64)
        w4_planes = keep.tile([P, 2 * N], U8, name="w4_planes", align_bytes=64)
        z_codes = keep.tile([P, 2 * M], U32, name="z_codes", align_bytes=64)
        z_planes = keep.tile([P, 2 * M], U8, name="z_planes", align_bytes=64)
        ident = keep.tile([P, P], F32, name="ident")
        pages = [keep.tile([P, T2], F32, name="page%d" % t) for t in range(2)]

        def load_planes(queue, tile, src):
            for q in range(4):
                queue.dma_start(
                    out=tile[32 * q : 32 * q + 4, :].bitcast(I32), in_=src[0, 4 * q : 4 * q + 4, :].bitcast(I32)
                )

        raw = {}

        def load_rows(key, rows, slot):
            width = rows.shape[1]
            raw[key] = slot_tile(slot, [P, PACK, width], F32, "raw_%s%d" % key)
            nc.sync.dma_start(out=raw[key][:], in_=rows.rearrange("(p i) w -> p i w", i=PACK))

        def round_rows(key, target, copy=nc.scalar.copy):
            copy(
                target.rearrange("p (c e i) -> p c i e", e=4, i=PACK),
                raw[key][:].rearrange("p i (c e) -> p c i e", e=4),
            )

        def quantise(codes, planes, col0, values, piece):
            total = values.shape[1] // PACK
            for done in range(0, total, piece):
                n = min(piece, total - done)
                cols = slice(col0 + done, col0 + done + n)
                nc.vector.quantize_mx(
                    out=codes[:, cols].bitcast(FP8X4),
                    scales=planes[:, cols],
                    in_=values[:, PACK * done : PACK * (done + n)],
                )

        w2_dram = w2_words[0].bitcast(I32)
        w3_dram = w3_words[0].rearrange("p c i -> p (c i)").bitcast(I32)

        def load_words(codes, dram, b):
            width = dram.shape[1] // 2
            cols = slice(b * width, (b + 1) * width)
            nc.sync.dma_start(out=codes[:].bitcast(I32)[:, cols], in_=dram[:, cols])

        def entries(lst, lo, hi):
            return lst[:, lo // PER_COL : hi // PER_COL]

        nc.gpsimd.memset(table_scales[:].bitcast(I32), 0)
        warm = slot_tile(0, [P, SLOT], F32, "warm")
        nc.gpsimd.memset(warm[:, 0:8], 0.0)
        make_identity(nc, ident[:])
        load_planes(nc.gpsimd, w2_planes, w2_scales)
        nc.gpsimd.memset(pages[0][:], 0.0)
        nc.gpsimd.memset(pages[1][:], 0.0)
        nc.sync.dma_start(list1[:], offs)
        nc.sync.dma_start(list2[:], offs2)
        nc.sync.dma_start(list3[:], offs3)
        table_words = slot_tile(8, [P, T], U32, "table_words")
        nc.sync.dma_start(
            out=table_words[:].bitcast(I32), in_=tab_words[0].rearrange("p t i -> p (t i)").bitcast(I32)
        )
        load_planes(nc.scalar, table_scales, tab_scales)
        nc.scalar.activation(out=warm[:, 8:9], in_=warm[:, 0:1], func=ACT.Tanh)

        w2_codes = slot_tile(0, [P, 2 * H], U8, "w2_codes")
        w3_codes = slot_tile(0.5, [P, H], U32, "w3_codes")
        w3_planes = slot_tile(1.5, [P, H], U8, "w3_planes")
        load_words(w2_codes, w2_dram, 0)
        load_rows(("w1", 0), w1[:, :CHUNK], 2)
        load_rows(("w1", 1), w1[:, CHUNK:BLOCK], 3)
        load_words(w3_codes, w3_dram, 0)
        load_planes(nc.sync, w3_planes, w3_scales)
        load_words(w2_codes, w2_dram, 1)
        load_words(w3_codes, w3_dram, 1)

        first = [slot_tile(slot, [P, PACK * CHUNK], BF16, "w1_values%d" % c) for c, slot in enumerate((4, 28.75))]
        round_rows(("w1", 0), first[0][:])
        round_rows(("w1", 1), first[1][:], nc.vector.tensor_copy)
        for c in range(2):
            quantise(w1_codes, w1_planes, c * CHUNK, first[c], CHUNK)

        v_words, v_scales = [], []

        def look_up(i, slot, word_slot):
            picked = entries(list1, i * BANK, (i + 1) * BANK)
            v_scales.append(slot_tile(slot, [P, BANK], U8, "v_scales%d" % i))
            v_words.append(slot_tile(word_slot, [P, BANK], U32, "v_words%d" % i))
            nc.vector.tensor_copy(v_scales[i][:], table_scales[:].indirect(picked))
            nc.vector.tensor_copy(v_words[i][:], table_words[:].indirect(picked))

        look_up(0, 5.25, 5.5)
        wgs_sb = slot_tile(3, [P, S], F32, "wgs_sb")
        gain_sb = slot_tile(4, [P, 2, PACK], F32, "gain_sb")
        nc.sync.dma_start(out=wgs_sb[:], in_=wgs)
        nc.sync.dma_start(out=gain_sb[:], in_=gain.rearrange("(b p t) -> p b t", b=2, t=PACK))
        pages.append(slot_tile(27, [P, T2], F32, "page2"))
        pages.append(slot_tile(29, [P, T2], F32, "page3"))
        nc.gpsimd.memset(pages[2][:], 0.0)
        nc.gpsimd.memset(pages[3][:], 0.0)

        h_rows = [slot_tile((20, 8)[b], [P, PACK, S], F32, "h_rows%d" % b) for b in range(2)]
        parts = {}

        def front(k):
            b, jt = divmod(k, 8)
            half, j0 = divmod(jt * P, BANK)
            stat = dict(lhsT=v_words[half][:, j0 : j0 + P].bitcast(FP8X4), lhsT_scale=v_scales[half][:, j0 : j0 + P])
            cols = slice(b * BLOCK, (b + 1) * BLOCK)
            sum_b = bank([P, BANK], "BZ"[k % 2], "sum_b")
            sum_c = bank([P, BANK], "CZ"[k % 2], "sum_c")
            sum_a = bank([P, BANK], "A", "sum_a")
            nc.tensor.matmul_mx(out=sum_b[:], rhs=w2_codes[:, 2 * b * BLOCK : 2 * (b + 1) * BLOCK].bitcast(FP4X4),
                                rhs_scale=w2_planes[:, cols], start=True, stop=True, **stat)
            nc.tensor.matmul_mx(out=sum_c[:], rhs=w3_codes[:, cols].bitcast(FP8X4), rhs_scale=w3_planes[:, cols],
                                start=True, stop=True, **stat)
            nc.tensor.matmul_mx(out=sum_a[:], rhs=w1_codes[:, cols].bitcast(FP8X4), rhs_scale=w1_planes[:, cols],
                                start=True, stop=True, **stat)
            if k < 2:
                neg_b = slot_tile(2 + k / 2, [P, PACK, P], F32, "neg_b%d" % k)
            elif k in ({11: 1, 13: 2, 15: 3}):
                neg_b = slot_tile(23 + ({11: 1, 13: 2, 15: 3})[k], [P, PACK, P], F32, "neg_b%d" % k)
            else:
                neg_b = ring.tile([P, PACK, P], F32, name="neg_b")
            if k == 1 or k == 2:
                abs_c = slot_tile(5 + k, [P, PACK, P], F32, "abs_c%d" % k)
            else:
                abs_c = ring.tile([P, PACK, P], F32, name="abs_c")
            neg_max = ring.tile([P, PACK, P], F32, name="neg_max")
            nc.scalar.activation(out=neg_b[:], in_=sum_b[:].rearrange("j (p t) -> j t p", t=PACK), func=ACT.Copy, scale=-1.0)
            nc.scalar.activation(out=abs_c[:], in_=sum_c[:].rearrange("j (p t) -> j t p", t=PACK), func=ACT.Abs)
            nc.vector.scalar_tensor_tensor(
                out=neg_max[:], in0=sum_a[:].rearrange("j (p t) -> j t p", t=PACK), in1=neg_b[:],
                scalar=-1.0,
                op0=ALU.mult, op1=ALU.min,
            )
            parts[k] = (abs_c, neg_max)

        def back(k):
            b, jt = divmod(k, 8)
            abs_c, neg_max = parts[k]
            neg_h = psum.tile([P, PACK, P], F32, name="neg_h", tag="H", bufs=2)
            for t in range(PACK):
                nc.tensor.matmul(neg_h[:, t, :], abs_c[:, t, :], ident[:], start=(t == 0), stop=False, is_transpose=True)
            for t in range(PACK):
                nc.tensor.matmul(neg_h[:, t, :], neg_max[:, t, :], ident[:], start=False, stop=(t == PACK - 1), is_transpose=True)
            nc.scalar.activation(out=h_rows[b][:, :, jt * P : (jt + 1) * P], in_=neg_h[:], func=ACT.Copy, scale=-1.0)

        def scatter(b, t, first, last, page):
            lo, hi = first * P, last * P
            nc.vector.tensor_tensor(
                pages[page][:].indirect(entries(list2, lo, hi)), h_rows[b][:, t, lo:hi], wgs_sb[:, lo:hi], ALU.mult
            )

        wear_sb = {}
        scaled = {}
        readings = {}
        tanhs = {}
        wear_rows = wear.rearrange("(b p t) m -> b t p m", b=2, t=PACK)

        def load_wear(b, t):
            wear_sb[b, t] = slot_tile((0, 1, 14, 15)[t], [P, M], F32, "wear%d%d" % (b, t))
            nc.sync.dma_start(out=wear_sb[b, t][:], in_=wear_rows[b, t])

        def read(b, t, lo, hi, page, apply_gain, behind=None):
            if lo == 0:
                if b == 0 and t in ({11: 1, 13: 2, 15: 3}).values():
                    readings[b, t] = slot_tile(23 + t, [P, M], F32, "x%d" % t)
                else:
                    readings[b, t] = ring.tile([P, M], F32, name="x", tag="x", bufs=2)
                if behind is None:
                    tanhs[b, t] = ring.tile([P, M], F32, name="bounded", tag="bounded", bufs=2)
                else:
                    tanhs[b, t] = slot_tile(16 + behind, [P, M], F32, "bounded%d%d" % (b, t))
            x = readings[b, t][:, lo:hi]
            bounded = tanhs[b, t][:, lo:hi]
            nc.vector.tensor_tensor(x[:], pages[page][:].indirect(entries(list3, lo, hi)), wgt_sb[:, lo:hi], ALU.mult)
            nc.scalar.activation(out=bounded[:], in_=x[:], func=ACT.Tanh)
            if apply_gain:
                scaled[b, t] = slot_tile(16 + t, [P, M], F32, "scaled%d%d" % (b, t))
                nc.scalar.activation(out=scaled[b, t][:], in_=bounded, func=ACT.Copy, scale=gain_sb[:, b, t : t + 1])

        turned = {}

        def add_wear(b, u, c):
            z_sum = bank([P, 2, 2, P], ("AABC", "HHAA", "BCAA")[2 * b + u][c], "z_sum")
            terms = [(source, e, mt) for source in (wear_sb, scaled) for e in range(2) for mt in range(2)]
            for n, (source, e, mt) in enumerate(terms):
                cols = slice(c * CHUNK + mt * P, c * CHUNK + (mt + 1) * P)
                nc.tensor.matmul(z_sum[:, mt, e, :], source[b, 2 * u + e][:, cols], ident[:],
                                 start=(n == 0), stop=(n == len(terms) - 1), is_transpose=True)
            turned[b, u, c] = ring.tile([P, BANK], BF16, name="turned", tag="turned", bufs=8)
            nc.scalar.copy(
                turned[b, u, c][:].rearrange("m (mt p e) -> m mt p e", mt=2, e=2),
                z_sum[:].rearrange("m mt e p -> m mt p e"),
            )

        def interleave(values, pairs):
            nc.scalar.copy(values.bitcast(F32).rearrange("p (m u) -> p m u", u=2), pairs[:].rearrange("p u m -> p m u"))

        def turn_pair(target, b, u, c):
            words = turned[b, u, c][:].bitcast(F32)
            for mt in range(2):
                nc.tensor.transpose(target[:, mt * P : (mt + 1) * P], words[:, mt * P : (mt + 1) * P], ident[:])

        def turn_back(b, c):
            pairs = bank([P, 2, CHUNK], "Z", "pairs")
            for u in range(2):
                turn_pair(pairs[:, u, :], b, u, c)
            interleave(z_first[:, c * PACK * CHUNK : (c + 1) * PACK * CHUNK], pairs)

        pieces = [(0,256),(256,512),(512,768),(768,1024)]
        last_pairs = {}

        def turn_back_first_pair(c):
            pair = bank([P, CHUNK], "HHZZ"[c], "pair")
            turn_pair(pair, 1, 0, c)
            for lo, hi in pieces:
                if lo // CHUNK == c:
                    last_pairs[lo] = ring.tile([P, 2, hi - lo], F32, name="last_pairs", tag="last_pairs", bufs=len(pieces))
                    nc.scalar.copy(last_pairs[lo][:, 0, :], pair[:, lo - c * CHUNK : hi - c * CHUNK])

        def finish_direct(t, lo, hi):
            halves = last_pairs[lo][:, 1, :].bitcast(BF16).rearrange("p (m e) -> p m e", e=2)
            nc.vector.scalar_tensor_tensor(
                out=halves[:, :, t - 2], in0=tanhs[1, t][:, lo:hi], scalar=gain_sb[:, 1, t : t + 1],
                in1=wear_sb[1, t][:, lo:hi], op0=ALU.mult, op1=ALU.add,
            )

        scores = {}
        out_rows = out.rearrange("(nt p) m -> p nt m", p=P)
        score_tags = list("BHCHAZAZ")

        def score_pass(b, lo, hi):
            per_bank = min(N // P, BANK // (hi - lo))
            if b == 0:
                scores[lo] = []
                for nt in range(0, N // P, per_bank):
                    count = min(per_bank, N // P - nt)
                    scores[lo].append((nt, count, bank([P, count, hi - lo], score_tags.pop(0), "score")))
            cols = slice(b * M + lo, b * M + hi)
            for first, count, sums in scores[lo]:
                for i in range(count):
                    w_cols = slice(b * N + (first + i) * P, b * N + (first + i + 1) * P)
                    nc.tensor.matmul_mx(
                        out=sums[:, i, :], lhsT=w4_codes[:, w_cols].bitcast(FP8X4), lhsT_scale=w4_planes[:, w_cols],
                        rhs=z_codes[:, cols].bitcast(FP8X4), rhs_scale=z_planes[:, cols],
                        start=(b == 0 and i == 0), stop=(b == 1 and i == count - 1),
                    )

        def store(lo, hi, copies):
            staged = ring.tile([P, N // P, hi - lo], F32, name="staged", tag="staged", bufs=len(pieces))
            for (first, count, sums), copy in zip(scores[lo], copies):
                copy(staged[:, first : first + count, :], sums[:])
            nc.sync.dma_start(out=out_rows[:, :, lo:hi], in_=staged[:])

        chunks = range(M // CHUNK)
        reads = {9: 0, 11: 1, 13: 2, 15: 3}
        put_up_to = {}

        def put(k, t):
            b, jt = divmod(k, 8)
            scatter(b, t, put_up_to.get((b, t), 0), jt + 1, (t + 2) % PACK)
            put_up_to[b, t] = jt + 1

        front(0)
        for k in range(16):
            if k < 15:
                front(k + 1)
            if k == 0:
                look_up(1, 2, 2.5)
                wgt_sb = slot_tile(13, [P, M], F32, "wgt_sb")
                nc.sync.dma_start(out=wgt_sb[:], in_=wgt)
            back(k)
            if k == 2:
                load_rows(("w1", 2), w1[:, BLOCK : BLOCK + CHUNK], 6)
                load_rows(("w1", 3), w1[:, BLOCK + CHUNK :], 7)
                second = slot_tile(15, [P, PACK * BLOCK], BF16, "w1_values2")
            if k == 4 or k == 5:
                round_rows(("w1", k - 2), second[:, (k - 4) * PACK * CHUNK : (k - 3) * PACK * CHUNK])
            if k == 5:
                quantise(w1_codes, w1_planes, BLOCK, second, BLOCK)
            if k in reads:
                read(0, reads[k], 0, M, (reads[k] + 2) % PACK, True)
            if k < 8:
                for t in ((2, 3) if k % 2 == 0 else (0, 1) if k < 7 else (0, 1, 2, 3)):
                    put(k, t)
            if k in ({9:0,11:1,13:0,14:1}):
                put(k, ({9:0,11:1,13:0,14:1})[k])
        put(15, 0)
        put(15, 1)
        for t in range(PACK):
            load_wear(0, t)
        w4_values = slot_tile(6, [P, 2 * PACK * N], BF16, "w4_values")
        for b in range(2):
            load_rows(("w4", b), w4[b * BLOCK : (b + 1) * BLOCK, :], 20 + 2 * b)
            round_rows(("w4", b), w4_values[:, b * PACK * N : (b + 1) * PACK * N])
        quantise(w4_codes, w4_planes, 0, w4_values, BLOCK)
        for c in chunks:
            add_wear(0, 0, c)
        load_wear(1, 0)
        load_wear(1, 1)
        z_first = slot_tile(24, [P, PACK * M], BF16, "z_first")
        for c in chunks:
            add_wear(0, 1, c)
            turn_back(0, c)
        load_wear(1, 2)
        load_wear(1, 3)
        read(1, 1, 0, M, 3, True, 3)
        scatter(1, 2, 0, 8, 3)
        quantise(z_codes, z_planes, 0, z_first, M)
        read(1, 0, 0, M, 2, True, 2)
        for c in chunks:
            add_wear(1, 0, c)
        read(1, 2, 0, M, 3, False, 1)
        for c in chunks:
            turn_back_first_pair(c)
        for lo, hi in pieces:
            score_pass(0, lo, hi)
        scatter(1, 3, 0, 8, 3)
        for lo, hi in pieces:
            read(1, 3, lo, hi, 3, False, 0)
        for n, (lo, hi) in enumerate(pieces):
            for t in (3,2):
                finish_direct(t, lo, hi)
            values = ring.tile([P, PACK * CHUNK], BF16, name="z_values", tag="z_values", bufs=4, align_bytes=64)
            interleave(values[:], last_pairs[lo])
            quantise(z_codes, z_planes, M + lo, values, CHUNK)
            score_pass(1, lo, hi)
        for n, (lo, hi) in enumerate(pieces):
            store(lo, hi, (nc.vector.tensor_copy, nc.scalar.copy))
